import numpy as np
import ml_dtypes


def mxq(x, axis, fmt="e4m3"):
    dtype, down = {"e4m3": (ml_dtypes.float8_e4m3fn, 7), "e5m2": (ml_dtypes.float8_e5m2, 14)}[fmt]
    v = np.moveaxis(np.asarray(x, np.float32).astype(ml_dtypes.bfloat16).astype(np.float64), axis, -1)
    blocks = v.reshape(v.shape[:-1] + (-1, 32))
    amax = np.abs(blocks).max(-1, keepdims=True)
    byte = np.maximum(np.where(amax > 0, np.frexp(amax)[1] - 1 + 127, 0) - down, 1)
    scale = np.exp2(byte - 127.0)
    codes = (blocks / scale).astype(np.float32).astype(dtype).astype(np.float64)
    return np.moveaxis((codes * scale).reshape(v.shape), -1, axis)


WIDE = False


def mx_kscale(k):
    if not WIDE:
        return np.ones(k)
    levels = np.array([10, -10, 5, -5, 0])
    if k % 512:
        return np.exp2(np.random.permutation(np.resize(levels, k // 32))).repeat(32)
    a = np.empty((k // 512, 16))
    for p in range(k // 512):
        a[p, :8] = np.random.permutation(np.resize(levels, 8))
        for g in range(8):
            far = levels[np.abs(levels - a[p, g]) >= 10]
            a[p, g + 8] = far[np.random.randint(len(far))]
    return np.exp2(a.ravel()).repeat(32)


BF16 = ml_dtypes.bfloat16


def bf(x):
    return np.asarray(x, np.float32).astype(BF16)


def f64(x):
    return np.asarray(x).astype(np.float64)


R, A, G = 1024, 2048, 1024


def setup_inputs():
    s, t = mx_kscale(A), mx_kscale(R)
    corridor = np.random.uniform(-1.2, 1.2, R)
    side = np.random.standard_normal(A)
    use = 0.4 * np.exp(corridor[:, None] * side) * np.random.uniform(0.5, 1.5, (R, A))
    link_len = np.random.uniform(0.5, 1.5, A) * 8.0 / A
    norm = 1.0 / np.sqrt((use * link_len).sum(1))
    taste = 2.0 * np.random.standard_normal((G, 1))
    share = np.exp(taste * corridor + np.random.standard_normal((G, R)))
    share = share / share.sum(1, keepdims=True)
    return {"scaled_inc": bf(use * link_len * s),
            "inc": bf(use / s),
            "row_norm": bf(norm * t),
            "col_norm": bf(norm),
            "share": bf(share / t)}


def reference(scaled_inc, inc, row_norm, col_norm, share):
    overlap = mxq(f64(scaled_inc), 1, "e4m3") @ mxq(f64(inc), 1, "e4m3").T
    c = overlap * f64(row_norm)[:, None]
    common = mxq(f64(share), 1, "e4m3") @ mxq(c, 0, "e4m3")
    return np.log(common * f64(col_norm))

@@ -1,0 +1,316 @@
+from contextlib import ExitStack
+
+import concourse.mybir as mybir
+from concourse.masks import make_identity
+
+R, A, G = 1024, 2048, 1024
+FLOPS = 2 * R * R * A + 2 * G * R * R
+
+F32 = mybir.dt.float32
+BF16 = mybir.dt.bfloat16
+U32 = mybir.dt.uint32
+U8 = mybir.dt.uint8
+FP8X4 = mybir.dt.float8_e4m3fn_x4
+MULT = mybir.AluOpType.mult
+LN = mybir.ActivationFunctionType.Ln
+
+P = 128
+WORDS = 1024
+QUARTER = 256
+PLAN = 3
+UNSORTED = 5
+SORT_AHEAD = 2
+SCALAR_SORTS = (14, 16, 18)
+VECTOR_SPILLS = ()
+TBANKS = 4
+WARM = 0
+WARM_FILL = ()
+DIRECT = 0
+NARROW = ((1, 0), (1, 1), (1, 2), (1, 3))
+WEAVE_SCALAR = 0
+LAG_Q = 2
+LAG_C = 2
+LAG_LOG = 1
+SPLIT_LAST = 0
+
+
+def plan():
+    def turn(*key):
+        return ("turn", key)
+
+    def overlap(g, j, slots=(0, 1, 2, 3)):
+        return ("overlap", g, j, slots)
+
+    def common(h, q):
+        return ("common", h, q)
+
+    s = []
+    if PLAN == 1:
+        s += [turn("inc", 0, 0), turn("sc", 0, 0), turn("inc", 0, 1), turn("sc", 0, 1)]
+        s += [turn("sc", 0, 2), overlap(0, 0, (0, 1)), turn("sc", 0, 3), turn("sc", 1, 0)]
+        s += [overlap(0, 0, (2,)), turn("sc", 1, 1), turn("sc", 1, 2), overlap(0, 0, (3,)), overlap(1, 0, (0,))]
+        s += [turn("sc", 1, 3), turn("inc", 1, 0), overlap(1, 0, (1,)), overlap(1, 0, (2,))]
+        s += [turn("inc", 1, 1), turn("share", 0), overlap(1, 0, (3,))]
+        for q in range(1, 4):
+            s += [overlap(0, q, (0, 1)), overlap(0, q, (2, 3)), common(q - 1, q - 1)]
+            if q < 3:
+                s += [turn("inc", q + 1, 0)]
+            s += [turn("share", q)]
+            s += [overlap(1, q, (0, 1)), overlap(1, q, (2, 3))]
+            if q < 3:
+                s += [turn("inc", q + 1, 1)]
+            s += [common(h, q - 1) for h in range(q - 1)]
+            s += [common(q, x) for x in range(q)]
+        s += [common(h, 3) for h in range(4)]
+    if PLAN == 2:
+        s += [turn("inc", 0, 0), turn("sc", 0, 0), turn("inc", 0, 1), turn("sc", 0, 1)]
+        s += [turn("sc", 0, 2), overlap(0, 0, (0, 1)), turn("sc", 0, 3), turn("inc", 1, 0)]
+        s += [overlap(0, 0, (2,)), turn("inc", 1, 1), turn("sc", 1, 0), overlap(0, 0, (3,)), overlap(0, 1, (0, 1))]
+        s += [turn("sc", 1, 1), turn("sc", 1, 2), overlap(0, 1, (2, 3)), overlap(1, 0, (0, 1))]
+        s += [turn("sc", 1, 3), turn("share", 0), overlap(1, 1, (0, 1)), overlap(1, 0, (2, 3))]
+        s += [turn("inc", 2, 0), turn("inc", 2, 1), overlap(1, 1, (2, 3)), common(0, 0)]
+        s += [turn("share", 1), turn("share", 2), overlap(0, 2, (0, 1)), common(0, 1), overlap(0, 2, (2, 3)), common(1, 0)]
+        s += [turn("inc", 3, 0), turn("inc", 3, 1), overlap(1, 2, (0, 1)), common(1, 1), overlap(1, 2, (2, 3)), common(2, 0)]
+        s += [turn("share", 3), overlap(0, 3, (0, 1)), common(2, 1), overlap(0, 3, (2, 3)), common(0, 2), overlap(1, 3, (0, 1)), common(1, 2), overlap(1, 3, (2, 3))]
+        s += [common(2, 2), common(3, 0), common(3, 1), common(3, 2)]
+        s += [common(h, 3) for h in range(4)]
+    if PLAN == 3:
+        s += [turn("inc", 0, 0), turn("sc", 0, 0), turn("inc", 0, 1), turn("sc", 0, 1), turn("sc", 0, 2)]
+        s += [overlap(0, 0, (0,)), overlap(0, 0, (1,)), turn("sc", 0, 3), turn("sc", 1, 0), overlap(0, 0, (2,))]
+        s += [turn("sc", 1, 1), turn("inc", 1, 0), overlap(0, 0, (3,)), overlap(1, 0, (0,))]
+        s += [turn("sc", 1, 2), turn("inc", 1, 1), overlap(1, 0, (1,))]
+        s += [turn("sc", 1, 3), turn("share", 0), overlap(1, 0, (2,)), overlap(0, 1, (0, 1))]
+        s += [turn("inc", 2, 0), turn("share", 1), overlap(1, 0, (3,)), overlap(0, 1, (2, 3)), overlap(1, 1, (0, 1))]
+        s += [turn("inc", 2, 1), turn("share", 2), overlap(1, 1, (2, 3)), common(0, 0), common(1, 0), overlap(0, 2, (0, 1)), common(0, 1), overlap(0, 2, (2, 3))]
+        s += [turn("inc", 3, 0), turn("inc", 3, 1), common(1, 1), overlap(1, 2, (0, 1)), common(2, 0), overlap(1, 2, (2, 3))]
+        s += [turn("share", 3), common(2, 1), overlap(0, 3, (0, 1)), common(0, 2), overlap(0, 3, (2, 3)), common(1, 2), overlap(1, 3, (0, 1)), common(2, 2), overlap(1, 3, (2, 3))]
+        s += [common(3, 0), common(3, 1), common(3, 2)]
+        s += [common(h, 3) for h in range(4)]
+    return s
+
+
+def tile_route_overlap_penalty_s7_kernel(tc, scaled_inc, inc, row_norm, col_norm, share, out):
+    nc = tc.nc
+    steps = plan()
+    turns = [step[1] for step in steps if step[0] == "turn"]
+
+    scaled_rows = scaled_inc.rearrange("(g m t) a -> g t m a", g=2, t=4)
+    inc_rows = inc.rearrange("(q e n) (h a) -> q h n e a", e=2, n=P, h=2)
+    share_rows = share.rearrange("(h p e) i -> h p (e i)", h=4, e=2)
+    out_rows = out.rearrange("(h p e) j -> h p e j", h=4, e=2)
+
+    def source(key):
+        if key[0] == "sc":
+            return scaled_rows[key[1], key[2]]
+        if key[0] == "inc":
+            return inc_rows[key[1], key[2]]
+        return share_rows[key[1]]
+
+    with ExitStack() as ctx:
+        keep = ctx.enter_context(tc.tile_pool(name="keep", bufs=1))
+        flow = ctx.enter_context(tc.tile_pool(name="flow", bufs=3))
+        psum = ctx.enter_context(tc.psum_pool(name="psum", bufs=4))
+        ctx.enter_context(tc.manual_schedule())
+
+        ident = keep.tile([P, P], F32, name="ident")
+        make_identity(nc, ident[:])
+        one = keep.tile([P, 1], F32, name="one")
+        nc.vector.memset(one[:], 1.0)
+        warm = keep.tile([P, 1], F32, name="warm")
+        nc.scalar.activation(out=warm[:], in_=one[:], func=LN)
+
+        if WARM:
+            ones = keep.tile([P, 2048], BF16, name="ones", align_bytes=64)
+            nc.vector.memset(ones[:], 1.0)
+            warm_codes = keep.tile([P, 512], U32, name="warm_codes", align_bytes=64)
+            warm_scales = keep.tile([P, 512], U8, name="warm_scales", align_bytes=64)
+            nc.vector.quantize_mx(out=warm_codes[:].bitcast(FP8X4), scales=warm_scales[:], in_=ones[:])
+
+        def warm_up(count):
+            bank = psum.tile([P, 512], F32, name="acc", bufs=8 - TBANKS)
+            for n in range(count):
+                nc.tensor.matmul_mx(out=bank[:], lhsT=warm_codes[:, :P].bitcast(FP8X4), lhsT_scale=warm_scales[:, :P],
+                                    rhs=warm_codes[:].bitcast(FP8X4), rhs_scale=warm_scales[:], start=True, stop=True)
+
+        if WARM:
+            warm_up(WARM)
+
+        raw, ordered, grouped, codes, scales = {}, {}, {}, {}, {}
+        row_gain = keep.tile([P, 2, 4], BF16, name="row_gain")
+        col_gain = keep.tile([P, R], BF16, name="col_gain")
+        for n, key in enumerate(turns):
+            raw[key] = keep.tile([P, 2 * WORDS], BF16, name="raw%d" % n, align_bytes=64)
+            if key[0] == "inc":
+                nc.sync.dma_start(out=raw[key][:].rearrange("p (e a) -> p e a", e=2), in_=source(key))
+            else:
+                nc.sync.dma_start(out=raw[key][:], in_=source(key))
+            if n == 5:
+                nc.sync.dma_start(out=row_gain[:], in_=row_norm.rearrange("(g m t) -> m g t", g=2, t=4))
+        nc.sync.dma_start(out=col_gain[:], in_=col_norm.partition_broadcast(P))
+
+        def sort(n):
+            key = turns[n]
+            ordered[key] = flow.tile([P, WORDS], F32, name="ordered", bufs=SORT_AHEAD + 1, align_bytes=64)
+            dst = ordered[key][:].rearrange("p (u c w) -> p c u w", u=2, w=4)
+            src = raw[key][:].bitcast(F32).rearrange("p (c w u) -> p c u w", u=2, w=4)
+            if n in SCALAR_SORTS:
+                nc.scalar.copy(out=dst, in_=src)
+            else:
+                nc.vector.tensor_copy(out=dst, in_=src)
+
+        def turn(key):
+            n = turns.index(key)
+            grouped[key] = flow.tile([P, 2 * WORDS], BF16, name="grouped", bufs=4, align_bytes=64)
+            for half in range(2):
+                bank = psum.tile([P, 2, 2 * P], F32, name="turned", bufs=TBANKS)
+                for c in range(2):
+                    s = 2 * c + half if key[0] == "inc" else 2 * half + c
+                    for u in range(2):
+                        if key in ordered:
+                            words = ordered[key][:, 512 * u + P * s : 512 * u + P * (s + 1)]
+                        else:
+                            words = raw[key][:].bitcast(F32)[:, 256 * s + u : 256 * (s + 1) : 2]
+                        nc.tensor.transpose(out=bank[:, u, P * c : P * (c + 1)], in_=words, identity=ident[:])
+                dst = grouped[key][:].bitcast(F32)[:, 512 * half : 512 * (half + 1)].rearrange("p (n u) -> p n u", u=2)
+                src = bank[:].rearrange("p u n -> p n u")
+                if (n, half) in VECTOR_SPILLS:
+                    nc.vector.tensor_copy(out=dst, in_=src)
+                else:
+                    nc.scalar.copy(out=dst, in_=src)
+
+        def quantize_input(key):
+            name = "_".join(str(part) for part in key)
+            codes[key] = keep.tile([P, 512], U32, name="codes_" + name, align_bytes=64)
+            scales[key] = keep.tile([P, 512], U8, name="scales_" + name, align_bytes=64)
+            nc.vector.quantize_mx(out=codes[key][:].bitcast(FP8X4), scales=scales[key][:], in_=grouped[key][:])
+
+        def multiply(acc, left, left_col, right, right_col, width, start, stop):
+            lc = slice(left_col, left_col + P)
+            rc = slice(right_col, right_col + width)
+            nc.tensor.matmul_mx(out=acc, lhsT=codes[left][:, lc].bitcast(FP8X4), lhsT_scale=scales[left][:, lc],
+                                rhs=codes[right][:, rc].bitcast(FP8X4), rhs_scale=scales[right][:, rc],
+                                start=start, stop=stop)
+
+        banks, c_pairs, c_values = {}, {}, {}
+
+        def overlap(g, q, slots):
+            if (g, q) in NARROW:
+                if len(slots) == 1:
+                    work = [(e, slots[0]) for e in range(2)]
+                else:
+                    work = [(slots[0] // 2, t) for t in range(4)]
+                for e, t in work:
+                    if t == 0:
+                        banks[g, q, e] = psum.tile([P, 4, P], F32, name="acc", bufs=8 - TBANKS)
+                    for s in range(4):
+                        multiply(banks[g, q, e][:, t, :], ("sc", g, t), P * s, ("inc", q, s // 2), QUARTER * (s % 2) + P * e, P, s == 0, s == 3)
+                return
+            for t in slots:
+                if t % 2 == 0:
+                    banks[g, q, t // 2] = psum.tile([P, 2, QUARTER], F32, name="acc", bufs=8 - TBANKS)
+                for s in range(4):
+                    multiply(banks[g, q, t // 2][:, t % 2, :], ("sc", g, t), P * s, ("inc", q, s // 2), QUARTER * (s % 2), QUARTER, s == 0, s == 3)
+
+        def scale_rows(g, q, u, slots):
+            if (g, q) in NARROW:
+                if len(slots) == 1 and u == 0:
+                    return
+                for e in range(2) if len(slots) == 1 else (u,):
+                    if e == 0:
+                        c_values[g, q] = flow.tile([P, QUARTER, 4], BF16, name="c_values", align_bytes=64)
+                    nc.vector.tensor_tensor(out=c_values[g, q][:, P * e : P * (e + 1), :], in0=banks[g, q, e][:].rearrange("p t n -> p n t"),
+                                            in1=row_gain[:, g, :].unsqueeze(1).to_broadcast([P, P, 4]), op=MULT)
+                return
+            gain = row_gain[:, g, 2 * u : 2 * u + 2].unsqueeze(1).to_broadcast([P, QUARTER, 2])
+            src = banks[g, q, u][:].rearrange("p e n -> p n e")
+            if DIRECT:
+                if u == 0:
+                    c_values[g, q] = flow.tile([P, QUARTER, 4], BF16, name="c_values", align_bytes=64)
+                nc.vector.tensor_tensor(out=c_values[g, q][:, :, 2 * u : 2 * u + 2], in0=src, in1=gain, op=MULT)
+            else:
+                if u == 0:
+                    c_pairs[g, q] = flow.tile([P, 2, QUARTER, 2], BF16, name="c_pairs", align_bytes=64)
+                nc.vector.tensor_tensor(out=c_pairs[g, q][:, u], in0=src, in1=gain, op=MULT)
+
+        def weave_c(g, q):
+            if not DIRECT and (g, q) not in NARROW:
+                c_values[g, q] = flow.tile([P, QUARTER, 4], BF16, name="c_values", align_bytes=64)
+                dst = c_values[g, q][:].rearrange("p n t -> p (n t)").bitcast(F32).rearrange("p (n u) -> p n u", u=2)
+                src = c_pairs[g, q][:].rearrange("p u n e -> p (u n e)").bitcast(F32).rearrange("p (u n) -> p n u", u=2)
+                if WEAVE_SCALAR:
+                    nc.scalar.copy(out=dst, in_=src)
+                else:
+                    nc.vector.tensor_copy(out=dst, in_=src)
+
+        def quantize_c(g, q):
+            key = ("c", g, q)
+            codes[key] = keep.tile([P, QUARTER], U32, name="c_codes%d_%d" % (g, q), align_bytes=64)
+            scales[key] = keep.tile([P, QUARTER], U8, name="c_scales%d_%d" % (g, q), align_bytes=64)
+            nc.vector.quantize_mx(out=codes[key][:].bitcast(FP8X4), scales=scales[key][:],
+                                  in_=c_values[g, q][:].rearrange("p n t -> p (n t)"))
+
+        products = {}
+
+        def common(h, q):
+            banks["o", h, q] = psum.tile([P, 2, QUARTER], F32, name="acc", bufs=8 - TBANKS)
+            for e in range(2):
+                for g in range(2):
+                    multiply(banks["o", h, q][:, e, :], ("share", h), P * (2 * e + g), ("c", g, q), 0, QUARTER, g == 0, g == 1)
+
+        def scale_columns(h, q):
+            products[h, q] = flow.tile([P, 2, QUARTER], F32, name="product", bufs=4)
+            gain = col_gain[:, QUARTER * q : QUARTER * (q + 1)].unsqueeze(1).to_broadcast([P, 2, QUARTER])
+            nc.vector.tensor_tensor(out=products[h, q][:], in0=banks["o", h, q][:], in1=gain, op=MULT)
+
+        def log_and_store(h, q):
+            result = flow.tile([P, 2, QUARTER], F32, name="result", bufs=8)
+            nc.scalar.activation(out=result[:], in_=products[h, q][:], func=LN)
+            nc.sync.dma_start(out=out_rows[h, :, :, QUARTER * q : QUARTER * (q + 1)], in_=result[:])
+
+        pending = []
+
+        def defer(due, made, action, *args):
+            pending.append((due, made, action, args))
+
+        def release(now, needed):
+            chain = [item[1][1:] for item in pending if item[1] in needed and item[1][0] == "c"]
+            for item in list(pending):
+                if item[0] <= now or item[1] in needed or (item[1][0] == "woven" and item[1][1:] in chain):
+                    pending.remove(item)
+                    item[2](*item[3])
+
+        sorted_upto = max(UNSORTED, 1)
+        if UNSORTED == 0:
+            sort(0)
+        for now, step in enumerate(steps):
+            if step[0] == "overlap":
+                g, q, slots = step[1:]
+                both = (g, q) in NARROW and len(slots) > 1
+                release(-1, [("sc", g, t) for t in (range(4) if both else slots)] + [("inc", q, 0), ("inc", q, 1)])
+                overlap(g, q, slots)
+            if step[0] == "common":
+                release(-1, [("share", step[1]), ("c", 0, step[2]), ("c", 1, step[2])])
+                common(step[1], step[2])
+            if step[0] == "turn":
+                turn(step[1])
+            release(now, [])
+            if step[0] == "turn":
+                defer(now + LAG_Q, step[1], quantize_input, step[1])
+                turned = turns.index(step[1]) + 1
+                if WARM and turns.index(step[1]) in WARM_FILL:
+                    warm_up(2)
+            if sorted_upto < min(turned + SORT_AHEAD, len(turns)) and (step[0] != "turn" or turned > UNSORTED):
+                sort(sorted_upto)
+                sorted_upto = sorted_upto + 1
+            if step[0] == "overlap" and slots[-1] % 2 == 1:
+                scale_rows(g, q, slots[-1] // 2, slots)
+            if step[0] == "overlap" and slots[-1] == 3:
+                if (g, q) in NARROW:
+                    defer(now + LAG_C, ("c", g, q), quantize_c, g, q)
+                else:
+                    defer(now + LAG_C, ("woven", g, q), weave_c, g, q)
+                    defer(now + LAG_C + 1, ("c", g, q), quantize_c, g, q)
+            if step[0] == "common":
+                scale_columns(step[1], step[2])
+                defer(now + LAG_LOG, ("out", step[1], step[2]), log_and_store, step[1], step[2])
+        release(len(steps) + 9, [])

@@ -18,20 +18,23 @@ P = 128
 WORDS = 1024
 QUARTER = 256
 PLAN = 3
-UNSORTED = 5
+UNSORTED = 1
+SKIP = (3, 6, 9)
 SORT_AHEAD = 2
-SCALAR_SORTS = (14, 16, 18)
+SCALAR_SORTS = (14, 15, 16, 17, 18, 19)
 VECTOR_SPILLS = ()
 TBANKS = 4
-WARM = 0
-WARM_FILL = ()
+WARM = 24
+HEAD = 5
+FILL = 6
+WARM_FILL = (1,)
 DIRECT = 0
 NARROW = ((1, 0), (1, 1), (1, 2), (1, 3))
 WEAVE_SCALAR = 0
 LAG_Q = 2
 LAG_C = 2
 LAG_LOG = 1
-SPLIT_LAST = 0
+SPLIT_LAST = 2
 
 
 def plan():
@@ -41,8 +44,8 @@ def plan():
     def overlap(g, j, slots=(0, 1, 2, 3)):
         return ("overlap", g, j, slots)
 
-    def common(h, q):
-        return ("common", h, q)
+    def common(h, q, half=None):
+        return ("common", h if isinstance(h, tuple) else (h,), q, half)
 
     s = []
     if PLAN == 1:
@@ -83,8 +86,55 @@ def plan():
         s += [turn("inc", 2, 0), turn("share", 1), overlap(1, 0, (3,)), overlap(0, 1, (2, 3)), overlap(1, 1, (0, 1))]
         s += [turn("inc", 2, 1), turn("share", 2), overlap(1, 1, (2, 3)), common(0, 0), common(1, 0), overlap(0, 2, (0, 1)), common(0, 1), overlap(0, 2, (2, 3))]
         s += [turn("inc", 3, 0), turn("inc", 3, 1), common(1, 1), overlap(1, 2, (0, 1)), common(2, 0), overlap(1, 2, (2, 3))]
-        s += [turn("share", 3), common(2, 1), overlap(0, 3, (0, 1)), common(0, 2), overlap(0, 3, (2, 3)), common(1, 2), overlap(1, 3, (0, 1)), common(2, 2), overlap(1, 3, (2, 3))]
-        s += [common(3, 0), common(3, 1), common(3, 2)]
+        s += [turn("share", 3), common(2, 1), overlap(0, 3, (0, 1)), common(0, 2), overlap(0, 3, (2, 3)), common(1, 2)]
+        if SPLIT_LAST == 0:
+            s += [overlap(1, 3, (0, 1)), common(2, 2), overlap(1, 3, (2, 3))]
+            s += [common(3, 0), common(3, 1), common(3, 2)]
+            s += [common(h, 3) for h in range(4)]
+        if SPLIT_LAST == 1:
+            s += [common(2, 2), overlap(1, 3, (0, 1)), common(3, 0), common(3, 1), overlap(1, 3, (2, 3)), common(3, 2)]
+            s += [common((0, 1), 3, 0), common((2, 3), 3, 0), common((0, 1), 3, 1), common(2, 3, 1), common(3, 3, 1)]
+        if SPLIT_LAST == 2:
+            s += [common(2, 2), common(3, 0), overlap(1, 3, (0, 1)), common(3, 1), overlap(1, 3, (2, 3)), common(3, 2)]
+            s += [common((0, 1), 3, 0), common((2, 3), 3, 0), common((0, 1), 3, 1), common(2, 3, 1), common(3, 3, 1)]
+        if SPLIT_LAST == 3:
+            s += [common(2, 2), overlap(1, 3, (0, 1)), common(3, 0), common(3, 1), common(3, 2), overlap(1, 3, (2, 3))]
+            s += [common((0, 1), 3, 0), common((2, 3), 3, 0), common((0, 1), 3, 1), common(2, 3, 1), common(3, 3, 1)]
+    if PLAN == 4:
+        s += [turn("inc", 0, 0), turn("sc", 0, 0), turn("inc", 0, 1), turn("inc", 1, 0), turn("inc", 1, 1)]
+        s += [overlap(0, 0, (0,)), turn("sc", 0, 1), turn("sc", 0, 2), overlap(0, 1, (0,))]
+        s += [turn("sc", 0, 3), turn("sc", 1, 0), overlap(0, 0, (1,)), overlap(0, 1, (1,)), overlap(0, 0, (2,)), overlap(0, 1, (2,))]
+        s += [turn("sc", 1, 1), turn("sc", 1, 2), overlap(0, 0, (3,)), overlap(0, 1, (3,)), overlap(1, 0, (0,)), overlap(1, 1, (0,))]
+        s += [turn("sc", 1, 3), turn("share", 0), overlap(1, 0, (1,)), overlap(1, 1, (1,)), overlap(1, 0, (2,)), overlap(1, 1, (2,))]
+        s += [turn("inc", 2, 0), turn("inc", 2, 1), overlap(1, 0, (3,)), overlap(1, 1, (3,))]
+        s += [turn("share", 1), overlap(0, 2, (0, 1)), common(0, 0), overlap(0, 2, (2, 3)), common(0, 1)]
+        s += [turn("inc", 3, 0), turn("inc", 3, 1), overlap(1, 2, (0, 1)), common(1, 0), overlap(1, 2, (2, 3)), common(1, 1)]
+        s += [turn("share", 2), turn("share", 3), overlap(0, 3, (0, 1)), common(0, 2), overlap(0, 3, (2, 3)), common(1, 2)]
+        s += [overlap(1, 3, (0, 1)), common(2, 0), common(2, 1), overlap(1, 3, (2, 3)), common(2, 2), common(3, 0), common(3, 1), common(3, 2)]
+        s += [common(h, 3) for h in range(4)]
+    if PLAN == 5:
+        s += [turn("inc", 0, 0), turn("sc", 0, 0), turn("inc", 0, 1), turn("sc", 0, 1), turn("inc", 1, 0)]
+        s += [overlap(0, 0, (0,)), turn("inc", 1, 1), turn("sc", 0, 2), overlap(0, 0, (1,))]
+        s += [turn("sc", 0, 3), turn("sc", 1, 0), overlap(0, 1, (0,)), overlap(0, 1, (1,)), overlap(0, 0, (2,)), overlap(0, 1, (2,))]
+        s += [turn("sc", 1, 1), turn("sc", 1, 2), overlap(0, 0, (3,)), overlap(0, 1, (3,)), overlap(1, 0, (0,)), overlap(1, 1, (0,))]
+        s += [turn("sc", 1, 3), turn("inc", 2, 0), overlap(1, 0, (1,)), overlap(1, 1, (1,)), overlap(1, 0, (2,)), overlap(1, 1, (2,))]
+        s += [turn("inc", 2, 1), turn("share", 0), overlap(1, 0, (3,)), overlap(1, 1, (3,)), overlap(0, 2, (0, 1))]
+        s += [turn("share", 1), turn("inc", 3, 0), overlap(0, 2, (2, 3)), common(0, 0), common(0, 1), overlap(1, 2, (0, 1))]
+        s += [turn("inc", 3, 1), turn("share", 2), overlap(1, 2, (2, 3)), common(1, 0), common(1, 1), overlap(0, 3, (0, 1)), common(0, 2)]
+        s += [turn("share", 3), overlap(0, 3, (2, 3)), common(1, 2), common(2, 0)]
+        s += [overlap(1, 3, (0, 1)), common(2, 1), common(2, 2), overlap(1, 3, (2, 3)), common(3, 0), common(3, 1), common(3, 2)]
+        s += [common(h, 3) for h in range(4)]
+    if PLAN == 6:
+        s += [turn("inc", 0, 0), turn("sc", 0, 0), turn("inc", 0, 1), turn("sc", 0, 1)]
+        s += [overlap(0, 0, (0,)), turn("sc", 0, 2), turn("sc", 0, 3), overlap(0, 0, (1,))]
+        s += [turn("sc", 1, 0), turn("inc", 1, 0), overlap(0, 0, (2,)), overlap(0, 0, (3,))]
+        s += [turn("sc", 1, 1), turn("inc", 1, 1), overlap(1, 0, (0,))]
+        s += [turn("sc", 1, 2), turn("sc", 1, 3), overlap(1, 0, (1,)), overlap(0, 1, (0, 1))]
+        s += [turn("share", 0), turn("inc", 2, 0), overlap(1, 0, (2,)), overlap(1, 0, (3,)), overlap(0, 1, (2, 3)), overlap(1, 1, (0, 1))]
+        s += [turn("inc", 2, 1), turn("share", 1), overlap(1, 1, (2, 3)), common(0, 0), overlap(0, 2, (0, 1)), common(0, 1), overlap(0, 2, (2, 3))]
+        s += [turn("inc", 3, 0), turn("inc", 3, 1), common(1, 0), overlap(1, 2, (0, 1)), common(1, 1), overlap(1, 2, (2, 3))]
+        s += [turn("share", 2), turn("share", 3), overlap(0, 3, (0, 1)), common(0, 2), overlap(0, 3, (2, 3)), common(1, 2), overlap(1, 3, (0, 1)), common(2, 0), common(2, 1), overlap(1, 3, (2, 3))]
+        s += [common(2, 2), common(3, 0), common(3, 1), common(3, 2)]
         s += [common(h, 3) for h in range(4)]
     return s
 
@@ -120,14 +170,14 @@ def tile_route_overlap_penalty_s7_kernel(tc, scaled_inc, inc, row_norm, col_norm
         nc.scalar.activation(out=warm[:], in_=one[:], func=LN)
 
         if WARM:
-            ones = keep.tile([P, 2048], BF16, name="ones", align_bytes=64)
+            ones = keep.tile([P, 512], BF16, name="ones", align_bytes=64)
             nc.vector.memset(ones[:], 1.0)
-            warm_codes = keep.tile([P, 512], U32, name="warm_codes", align_bytes=64)
-            warm_scales = keep.tile([P, 512], U8, name="warm_scales", align_bytes=64)
+            warm_codes = keep.tile([P, P], U32, name="warm_codes", align_bytes=64)
+            warm_scales = keep.tile([P, P], U8, name="warm_scales", align_bytes=64)
             nc.vector.quantize_mx(out=warm_codes[:].bitcast(FP8X4), scales=warm_scales[:], in_=ones[:])
 
         def warm_up(count):
-            bank = psum.tile([P, 512], F32, name="acc", bufs=8 - TBANKS)
+            bank = psum.tile([P, P], F32, name="acc", bufs=8 - TBANKS)
             for n in range(count):
                 nc.tensor.matmul_mx(out=bank[:], lhsT=warm_codes[:, :P].bitcast(FP8X4), lhsT_scale=warm_scales[:, :P],
                                     rhs=warm_codes[:].bitcast(FP8X4), rhs_scale=warm_scales[:], start=True, stop=True)
@@ -242,30 +292,44 @@ def tile_route_overlap_penalty_s7_kernel(tc, scaled_inc, inc, row_norm, col_norm
                 else:
                     nc.vector.tensor_copy(out=dst, in_=src)
 
-        def quantize_c(g, q):
-            key = ("c", g, q)
-            codes[key] = keep.tile([P, QUARTER], U32, name="c_codes%d_%d" % (g, q), align_bytes=64)
-            scales[key] = keep.tile([P, QUARTER], U8, name="c_scales%d_%d" % (g, q), align_bytes=64)
+        def quantize_c(g, q, half):
+            key = ("c", g, q) if half is None else ("c", g, q, half)
+            width = QUARTER if half is None else P
+            codes[key] = keep.tile([P, width], U32, name="c_codes%d_%d_%s" % (g, q, half), align_bytes=64)
+            scales[key] = keep.tile([P, width], U8, name="c_scales%d_%d_%s" % (g, q, half), align_bytes=64)
+            cols = slice(0, QUARTER) if half is None else slice(P * half, P * (half + 1))
             nc.vector.quantize_mx(out=codes[key][:].bitcast(FP8X4), scales=scales[key][:],
-                                  in_=c_values[g, q][:].rearrange("p n t -> p (n t)"))
+                                  in_=c_values[g, q][:, cols, :].rearrange("p n t -> p (n t)"))
 
         products = {}
 
-        def common(h, q):
-            banks["o", h, q] = psum.tile([P, 2, QUARTER], F32, name="acc", bufs=8 - TBANKS)
-            for e in range(2):
-                for g in range(2):
-                    multiply(banks["o", h, q][:, e, :], ("share", h), P * (2 * e + g), ("c", g, q), 0, QUARTER, g == 0, g == 1)
+        def common(hs, q, half):
+            width = QUARTER if half is None else P
+            first = 0 if half is None else P * half
+            bank = psum.tile([P, 2 * len(hs), width], F32, name="acc", bufs=8 - TBANKS)
+            for n, h in enumerate(hs):
+                for e in range(2):
+                    for g in range(2):
+                        if ("c", g, q) in codes:
+                            multiply(bank[:, 2 * n + e, :], ("share", h), P * (2 * e + g), ("c", g, q), first, width, g == 0, g == 1)
+                        else:
+                            multiply(bank[:, 2 * n + e, :], ("share", h), P * (2 * e + g), ("c", g, q, half), 0, width, g == 0, g == 1)
+            banks[hs, q, half] = bank
 
-        def scale_columns(h, q):
-            products[h, q] = flow.tile([P, 2, QUARTER], F32, name="product", bufs=4)
-            gain = col_gain[:, QUARTER * q : QUARTER * (q + 1)].unsqueeze(1).to_broadcast([P, 2, QUARTER])
-            nc.vector.tensor_tensor(out=products[h, q][:], in0=banks["o", h, q][:], in1=gain, op=MULT)
+        def scale_columns(hs, q, half):
+            width = QUARTER if half is None else P
+            first = QUARTER * q + (0 if half is None else P * half)
+            products[hs, q, half] = flow.tile([P, 2 * len(hs), width], F32, name="product", bufs=4)
+            gain = col_gain[:, first : first + width].unsqueeze(1).to_broadcast([P, 2 * len(hs), width])
+            nc.vector.tensor_tensor(out=products[hs, q, half][:], in0=banks[hs, q, half][:], in1=gain, op=MULT)
 
-        def log_and_store(h, q):
-            result = flow.tile([P, 2, QUARTER], F32, name="result", bufs=8)
-            nc.scalar.activation(out=result[:], in_=products[h, q][:], func=LN)
-            nc.sync.dma_start(out=out_rows[h, :, :, QUARTER * q : QUARTER * (q + 1)], in_=result[:])
+        def log_and_store(hs, q, half):
+            width = QUARTER if half is None else P
+            first = QUARTER * q + (0 if half is None else P * half)
+            result = flow.tile([P, 2 * len(hs), width], F32, name="result", bufs=8)
+            nc.scalar.activation(out=result[:], in_=products[hs, q, half][:], func=LN)
+            for n, h in enumerate(hs):
+                nc.sync.dma_start(out=out_rows[h, :, :, first : first + width], in_=result[:, 2 * n : 2 * n + 2, :])
 
         pending = []
 
@@ -289,8 +353,8 @@ def tile_route_overlap_penalty_s7_kernel(tc, scaled_inc, inc, row_norm, col_norm
                 release(-1, [("sc", g, t) for t in (range(4) if both else slots)] + [("inc", q, 0), ("inc", q, 1)])
                 overlap(g, q, slots)
             if step[0] == "common":
-                release(-1, [("share", step[1]), ("c", 0, step[2]), ("c", 1, step[2])])
-                common(step[1], step[2])
+                release(-1, [("share", h) for h in step[1]] + [("c", 0, step[2]), ("c", 1, step[2]), ("c", 1, step[2], step[3])])
+                common(step[1], step[2], step[3])
             if step[0] == "turn":
                 turn(step[1])
             release(now, [])
@@ -298,19 +362,25 @@ def tile_route_overlap_penalty_s7_kernel(tc, scaled_inc, inc, row_norm, col_norm
                 defer(now + LAG_Q, step[1], quantize_input, step[1])
                 turned = turns.index(step[1]) + 1
                 if WARM and turns.index(step[1]) in WARM_FILL:
-                    warm_up(2)
-            if sorted_upto < min(turned + SORT_AHEAD, len(turns)) and (step[0] != "turn" or turned > UNSORTED):
-                sort(sorted_upto)
+                    warm_up(FILL)
+            sorted_upto = max(sorted_upto, turned)
+            while sorted_upto in SKIP:
+                sorted_upto = sorted_upto + 1
+            if sorted_upto < min(turned + (1 if turned < HEAD else SORT_AHEAD), len(turns)) and (step[0] != "turn" or ((turned > UNSORTED or WARM) and sorted_upto not in SCALAR_SORTS)):
+                if sorted_upto not in SKIP:
+                    sort(sorted_upto)
                 sorted_upto = sorted_upto + 1
             if step[0] == "overlap" and slots[-1] % 2 == 1:
                 scale_rows(g, q, slots[-1] // 2, slots)
-            if step[0] == "overlap" and slots[-1] == 3:
+            if step[0] == "overlap" and SPLIT_LAST and (g, q) == (1, 3):
+                defer(now + LAG_C, ("c", g, q, slots[-1] // 2), quantize_c, g, q, slots[-1] // 2)
+            elif step[0] == "overlap" and slots[-1] == 3:
                 if (g, q) in NARROW:
-                    defer(now + LAG_C, ("c", g, q), quantize_c, g, q)
+                    defer(now + LAG_C, ("c", g, q), quantize_c, g, q, None)
                 else:
                     defer(now + LAG_C, ("woven", g, q), weave_c, g, q)
-                    defer(now + LAG_C + 1, ("c", g, q), quantize_c, g, q)
+                    defer(now + LAG_C + 1, ("c", g, q), quantize_c, g, q, None)
             if step[0] == "common":
-                scale_columns(step[1], step[2])
-                defer(now + LAG_LOG, ("out", step[1], step[2]), log_and_store, step[1], step[2])
+                scale_columns(step[1], step[2], step[3])
+                defer(now + LAG_LOG, ("out",) + step[1:], log_and_store, step[1], step[2], step[3])
         release(len(steps) + 9, [])

from contextlib import ExitStack

import concourse.mybir as mybir
from concourse.masks import make_identity

R, A, G = 1024, 2048, 1024
FLOPS = 2 * R * R * A + 2 * G * R * R

F32 = mybir.dt.float32
BF16 = mybir.dt.bfloat16
U32 = mybir.dt.uint32
U8 = mybir.dt.uint8
FP8X4 = mybir.dt.float8_e4m3fn_x4
MULT = mybir.AluOpType.mult
LN = mybir.ActivationFunctionType.Ln

P = 128
WORDS = 1024
QUARTER = 256
PLAN = 3
UNSORTED = 1
SKIP = (3, 6, 9)
SORT_AHEAD = 2
SCALAR_SORTS = (14, 15, 16, 17, 18, 19)
VECTOR_SPILLS = ()
TBANKS = 4
WARM = 24
HEAD = 5
FILL = 6
WARM_FILL = (1,)
DIRECT = 0
NARROW = ((1, 0), (1, 1), (1, 2), (1, 3))
WEAVE_SCALAR = 0
LAG_Q = 2
LAG_C = 2
LAG_LOG = 1
SPLIT_LAST = 2


def plan():
    def turn(*key):
        return ("turn", key)

    def overlap(g, j, slots=(0, 1, 2, 3)):
        return ("overlap", g, j, slots)

    def common(h, q, half=None):
        return ("common", h if isinstance(h, tuple) else (h,), q, half)

    s = []
    if PLAN == 1:
        s += [turn("inc", 0, 0), turn("sc", 0, 0), turn("inc", 0, 1), turn("sc", 0, 1)]
        s += [turn("sc", 0, 2), overlap(0, 0, (0, 1)), turn("sc", 0, 3), turn("sc", 1, 0)]
        s += [overlap(0, 0, (2,)), turn("sc", 1, 1), turn("sc", 1, 2), overlap(0, 0, (3,)), overlap(1, 0, (0,))]
        s += [turn("sc", 1, 3), turn("inc", 1, 0), overlap(1, 0, (1,)), overlap(1, 0, (2,))]
        s += [turn("inc", 1, 1), turn("share", 0), overlap(1, 0, (3,))]
        for q in range(1, 4):
            s += [overlap(0, q, (0, 1)), overlap(0, q, (2, 3)), common(q - 1, q - 1)]
            if q < 3:
                s += [turn("inc", q + 1, 0)]
            s += [turn("share", q)]
            s += [overlap(1, q, (0, 1)), overlap(1, q, (2, 3))]
            if q < 3:
                s += [turn("inc", q + 1, 1)]
            s += [common(h, q - 1) for h in range(q - 1)]
            s += [common(q, x) for x in range(q)]
        s += [common(h, 3) for h in range(4)]
    if PLAN == 2:
        s += [turn("inc", 0, 0), turn("sc", 0, 0), turn("inc", 0, 1), turn("sc", 0, 1)]
        s += [turn("sc", 0, 2), overlap(0, 0, (0, 1)), turn("sc", 0, 3), turn("inc", 1, 0)]
        s += [overlap(0, 0, (2,)), turn("inc", 1, 1), turn("sc", 1, 0), overlap(0, 0, (3,)), overlap(0, 1, (0, 1))]
        s += [turn("sc", 1, 1), turn("sc", 1, 2), overlap(0, 1, (2, 3)), overlap(1, 0, (0, 1))]
        s += [turn("sc", 1, 3), turn("share", 0), overlap(1, 1, (0, 1)), overlap(1, 0, (2, 3))]
        s += [turn("inc", 2, 0), turn("inc", 2, 1), overlap(1, 1, (2, 3)), common(0, 0)]
        s += [turn("share", 1), turn("share", 2), overlap(0, 2, (0, 1)), common(0, 1), overlap(0, 2, (2, 3)), common(1, 0)]
        s += [turn("inc", 3, 0), turn("inc", 3, 1), overlap(1, 2, (0, 1)), common(1, 1), overlap(1, 2, (2, 3)), common(2, 0)]
        s += [turn("share", 3), overlap(0, 3, (0, 1)), common(2, 1), overlap(0, 3, (2, 3)), common(0, 2), overlap(1, 3, (0, 1)), common(1, 2), overlap(1, 3, (2, 3))]
        s += [common(2, 2), common(3, 0), common(3, 1), common(3, 2)]
        s += [common(h, 3) for h in range(4)]
    if PLAN == 3:
        s += [turn("inc", 0, 0), turn("sc", 0, 0), turn("inc", 0, 1), turn("sc", 0, 1), turn("sc", 0, 2)]
        s += [overlap(0, 0, (0,)), overlap(0, 0, (1,)), turn("sc", 0, 3), turn("sc", 1, 0), overlap(0, 0, (2,))]
        s += [turn("sc", 1, 1), turn("inc", 1, 0), overlap(0, 0, (3,)), overlap(1, 0, (0,))]
        s += [turn("sc", 1, 2), turn("inc", 1, 1), overlap(1, 0, (1,))]
        s += [turn("sc", 1, 3), turn("share", 0), overlap(1, 0, (2,)), overlap(0, 1, (0, 1))]
        s += [turn("inc", 2, 0), turn("share", 1), overlap(1, 0, (3,)), overlap(0, 1, (2, 3)), overlap(1, 1, (0, 1))]
        s += [turn("inc", 2, 1), turn("share", 2), overlap(1, 1, (2, 3)), common(0, 0), common(1, 0), overlap(0, 2, (0, 1)), common(0, 1), overlap(0, 2, (2, 3))]
        s += [turn("inc", 3, 0), turn("inc", 3, 1), common(1, 1), overlap(1, 2, (0, 1)), common(2, 0), overlap(1, 2, (2, 3))]
        s += [turn("share", 3), common(2, 1), overlap(0, 3, (0, 1)), common(0, 2), overlap(0, 3, (2, 3)), common(1, 2)]
        if SPLIT_LAST == 0:
            s += [overlap(1, 3, (0, 1)), common(2, 2), overlap(1, 3, (2, 3))]
            s += [common(3, 0), common(3, 1), common(3, 2)]
            s += [common(h, 3) for h in range(4)]
        if SPLIT_LAST == 1:
            s += [common(2, 2), overlap(1, 3, (0, 1)), common(3, 0), common(3, 1), overlap(1, 3, (2, 3)), common(3, 2)]
            s += [common((0, 1), 3, 0), common((2, 3), 3, 0), common((0, 1), 3, 1), common(2, 3, 1), common(3, 3, 1)]
        if SPLIT_LAST == 2:
            s += [common(2, 2), common(3, 0), overlap(1, 3, (0, 1)), common(3, 1), overlap(1, 3, (2, 3)), common(3, 2)]
            s += [common((0, 1), 3, 0), common((2, 3), 3, 0), common((0, 1), 3, 1), common(2, 3, 1), common(3, 3, 1)]
        if SPLIT_LAST == 3:
            s += [common(2, 2), overlap(1, 3, (0, 1)), common(3, 0), common(3, 1), common(3, 2), overlap(1, 3, (2, 3))]
            s += [common((0, 1), 3, 0), common((2, 3), 3, 0), common((0, 1), 3, 1), common(2, 3, 1), common(3, 3, 1)]
    if PLAN == 4:
        s += [turn("inc", 0, 0), turn("sc", 0, 0), turn("inc", 0, 1), turn("inc", 1, 0), turn("inc", 1, 1)]
        s += [overlap(0, 0, (0,)), turn("sc", 0, 1), turn("sc", 0, 2), overlap(0, 1, (0,))]
        s += [turn("sc", 0, 3), turn("sc", 1, 0), overlap(0, 0, (1,)), overlap(0, 1, (1,)), overlap(0, 0, (2,)), overlap(0, 1, (2,))]
        s += [turn("sc", 1, 1), turn("sc", 1, 2), overlap(0, 0, (3,)), overlap(0, 1, (3,)), overlap(1, 0, (0,)), overlap(1, 1, (0,))]
        s += [turn("sc", 1, 3), turn("share", 0), overlap(1, 0, (1,)), overlap(1, 1, (1,)), overlap(1, 0, (2,)), overlap(1, 1, (2,))]
        s += [turn("inc", 2, 0), turn("inc", 2, 1), overlap(1, 0, (3,)), overlap(1, 1, (3,))]
        s += [turn("share", 1), overlap(0, 2, (0, 1)), common(0, 0), overlap(0, 2, (2, 3)), common(0, 1)]
        s += [turn("inc", 3, 0), turn("inc", 3, 1), overlap(1, 2, (0, 1)), common(1, 0), overlap(1, 2, (2, 3)), common(1, 1)]
        s += [turn("share", 2), turn("share", 3), overlap(0, 3, (0, 1)), common(0, 2), overlap(0, 3, (2, 3)), common(1, 2)]
        s += [overlap(1, 3, (0, 1)), common(2, 0), common(2, 1), overlap(1, 3, (2, 3)), common(2, 2), common(3, 0), common(3, 1), common(3, 2)]
        s += [common(h, 3) for h in range(4)]
    if PLAN == 5:
        s += [turn("inc", 0, 0), turn("sc", 0, 0), turn("inc", 0, 1), turn("sc", 0, 1), turn("inc", 1, 0)]
        s += [overlap(0, 0, (0,)), turn("inc", 1, 1), turn("sc", 0, 2), overlap(0, 0, (1,))]
        s += [turn("sc", 0, 3), turn("sc", 1, 0), overlap(0, 1, (0,)), overlap(0, 1, (1,)), overlap(0, 0, (2,)), overlap(0, 1, (2,))]
        s += [turn("sc", 1, 1), turn("sc", 1, 2), overlap(0, 0, (3,)), overlap(0, 1, (3,)), overlap(1, 0, (0,)), overlap(1, 1, (0,))]
        s += [turn("sc", 1, 3), turn("inc", 2, 0), overlap(1, 0, (1,)), overlap(1, 1, (1,)), overlap(1, 0, (2,)), overlap(1, 1, (2,))]
        s += [turn("inc", 2, 1), turn("share", 0), overlap(1, 0, (3,)), overlap(1, 1, (3,)), overlap(0, 2, (0, 1))]
        s += [turn("share", 1), turn("inc", 3, 0), overlap(0, 2, (2, 3)), common(0, 0), common(0, 1), overlap(1, 2, (0, 1))]
        s += [turn("inc", 3, 1), turn("share", 2), overlap(1, 2, (2, 3)), common(1, 0), common(1, 1), overlap(0, 3, (0, 1)), common(0, 2)]
        s += [turn("share", 3), overlap(0, 3, (2, 3)), common(1, 2), common(2, 0)]
        s += [overlap(1, 3, (0, 1)), common(2, 1), common(2, 2), overlap(1, 3, (2, 3)), common(3, 0), common(3, 1), common(3, 2)]
        s += [common(h, 3) for h in range(4)]
    if PLAN == 6:
        s += [turn("inc", 0, 0), turn("sc", 0, 0), turn("inc", 0, 1), turn("sc", 0, 1)]
        s += [overlap(0, 0, (0,)), turn("sc", 0, 2), turn("sc", 0, 3), overlap(0, 0, (1,))]
        s += [turn("sc", 1, 0), turn("inc", 1, 0), overlap(0, 0, (2,)), overlap(0, 0, (3,))]
        s += [turn("sc", 1, 1), turn("inc", 1, 1), overlap(1, 0, (0,))]
        s += [turn("sc", 1, 2), turn("sc", 1, 3), overlap(1, 0, (1,)), overlap(0, 1, (0, 1))]
        s += [turn("share", 0), turn("inc", 2, 0), overlap(1, 0, (2,)), overlap(1, 0, (3,)), overlap(0, 1, (2, 3)), overlap(1, 1, (0, 1))]
        s += [turn("inc", 2, 1), turn("share", 1), overlap(1, 1, (2, 3)), common(0, 0), overlap(0, 2, (0, 1)), common(0, 1), overlap(0, 2, (2, 3))]
        s += [turn("inc", 3, 0), turn("inc", 3, 1), common(1, 0), overlap(1, 2, (0, 1)), common(1, 1), overlap(1, 2, (2, 3))]
        s += [turn("share", 2), turn("share", 3), overlap(0, 3, (0, 1)), common(0, 2), overlap(0, 3, (2, 3)), common(1, 2), overlap(1, 3, (0, 1)), common(2, 0), common(2, 1), overlap(1, 3, (2, 3))]
        s += [common(2, 2), common(3, 0), common(3, 1), common(3, 2)]
        s += [common(h, 3) for h in range(4)]
    return s


def tile_route_overlap_penalty_s7_kernel(tc, scaled_inc, inc, row_norm, col_norm, share, out):
    nc = tc.nc
    steps = plan()
    turns = [step[1] for step in steps if step[0] == "turn"]

    scaled_rows = scaled_inc.rearrange("(g m t) a -> g t m a", g=2, t=4)
    inc_rows = inc.rearrange("(q e n) (h a) -> q h n e a", e=2, n=P, h=2)
    share_rows = share.rearrange("(h p e) i -> h p (e i)", h=4, e=2)
    out_rows = out.rearrange("(h p e) j -> h p e j", h=4, e=2)

    def source(key):
        if key[0] == "sc":
            return scaled_rows[key[1], key[2]]
        if key[0] == "inc":
            return inc_rows[key[1], key[2]]
        return share_rows[key[1]]

    with ExitStack() as ctx:
        keep = ctx.enter_context(tc.tile_pool(name="keep", bufs=1))
        flow = ctx.enter_context(tc.tile_pool(name="flow", bufs=3))
        psum = ctx.enter_context(tc.psum_pool(name="psum", bufs=4))
        ctx.enter_context(tc.manual_schedule())

        ident = keep.tile([P, P], F32, name="ident")
        make_identity(nc, ident[:])
        one = keep.tile([P, 1], F32, name="one")
        nc.vector.memset(one[:], 1.0)
        warm = keep.tile([P, 1], F32, name="warm")
        nc.scalar.activation(out=warm[:], in_=one[:], func=LN)

        if WARM:
            ones = keep.tile([P, 512], BF16, name="ones", align_bytes=64)
            nc.vector.memset(ones[:], 1.0)
            warm_codes = keep.tile([P, P], U32, name="warm_codes", align_bytes=64)
            warm_scales = keep.tile([P, P], U8, name="warm_scales", align_bytes=64)
            nc.vector.quantize_mx(out=warm_codes[:].bitcast(FP8X4), scales=warm_scales[:], in_=ones[:])

        def warm_up(count):
            bank = psum.tile([P, P], F32, name="acc", bufs=8 - TBANKS)
            for n in range(count):
                nc.tensor.matmul_mx(out=bank[:], lhsT=warm_codes[:, :P].bitcast(FP8X4), lhsT_scale=warm_scales[:, :P],
                                    rhs=warm_codes[:].bitcast(FP8X4), rhs_scale=warm_scales[:], start=True, stop=True)

        if WARM:
            warm_up(WARM)

        raw, ordered, grouped, codes, scales = {}, {}, {}, {}, {}
        row_gain = keep.tile([P, 2, 4], BF16, name="row_gain")
        col_gain = keep.tile([P, R], BF16, name="col_gain")
        for n, key in enumerate(turns):
            raw[key] = keep.tile([P, 2 * WORDS], BF16, name="raw%d" % n, align_bytes=64)
            if key[0] == "inc":
                nc.sync.dma_start(out=raw[key][:].rearrange("p (e a) -> p e a", e=2), in_=source(key))
            else:
                nc.sync.dma_start(out=raw[key][:], in_=source(key))
            if n == 5:
                nc.sync.dma_start(out=row_gain[:], in_=row_norm.rearrange("(g m t) -> m g t", g=2, t=4))
        nc.sync.dma_start(out=col_gain[:], in_=col_norm.partition_broadcast(P))

        def sort(n):
            key = turns[n]
            ordered[key] = flow.tile([P, WORDS], F32, name="ordered", bufs=SORT_AHEAD + 1, align_bytes=64)
            dst = ordered[key][:].rearrange("p (u c w) -> p c u w", u=2, w=4)
            src = raw[key][:].bitcast(F32).rearrange("p (c w u) -> p c u w", u=2, w=4)
            if n in SCALAR_SORTS:
                nc.scalar.copy(out=dst, in_=src)
            else:
                nc.vector.tensor_copy(out=dst, in_=src)

        def turn(key):
            n = turns.index(key)
            grouped[key] = flow.tile([P, 2 * WORDS], BF16, name="grouped", bufs=4, align_bytes=64)
            for half in range(2):
                bank = psum.tile([P, 2, 2 * P], F32, name="turned", bufs=TBANKS)
                for c in range(2):
                    s = 2 * c + half if key[0] == "inc" else 2 * half + c
                    for u in range(2):
                        if key in ordered:
                            words = ordered[key][:, 512 * u + P * s : 512 * u + P * (s + 1)]
                        else:
                            words = raw[key][:].bitcast(F32)[:, 256 * s + u : 256 * (s + 1) : 2]
                        nc.tensor.transpose(out=bank[:, u, P * c : P * (c + 1)], in_=words, identity=ident[:])
                dst = grouped[key][:].bitcast(F32)[:, 512 * half : 512 * (half + 1)].rearrange("p (n u) -> p n u", u=2)
                src = bank[:].rearrange("p u n -> p n u")
                if (n, half) in VECTOR_SPILLS:
                    nc.vector.tensor_copy(out=dst, in_=src)
                else:
                    nc.scalar.copy(out=dst, in_=src)

        def quantize_input(key):
            name = "_".join(str(part) for part in key)
            codes[key] = keep.tile([P, 512], U32, name="codes_" + name, align_bytes=64)
            scales[key] = keep.tile([P, 512], U8, name="scales_" + name, align_bytes=64)
            nc.vector.quantize_mx(out=codes[key][:].bitcast(FP8X4), scales=scales[key][:], in_=grouped[key][:])

        def multiply(acc, left, left_col, right, right_col, width, start, stop):
            lc = slice(left_col, left_col + P)
            rc = slice(right_col, right_col + width)
            nc.tensor.matmul_mx(out=acc, lhsT=codes[left][:, lc].bitcast(FP8X4), lhsT_scale=scales[left][:, lc],
                                rhs=codes[right][:, rc].bitcast(FP8X4), rhs_scale=scales[right][:, rc],
                                start=start, stop=stop)

        banks, c_pairs, c_values = {}, {}, {}

        def overlap(g, q, slots):
            if (g, q) in NARROW:
                if len(slots) == 1:
                    work = [(e, slots[0]) for e in range(2)]
                else:
                    work = [(slots[0] // 2, t) for t in range(4)]
                for e, t in work:
                    if t == 0:
                        banks[g, q, e] = psum.tile([P, 4, P], F32, name="acc", bufs=8 - TBANKS)
                    for s in range(4):
                        multiply(banks[g, q, e][:, t, :], ("sc", g, t), P * s, ("inc", q, s // 2), QUARTER * (s % 2) + P * e, P, s == 0, s == 3)
                return
            for t in slots:
                if t % 2 == 0:
                    banks[g, q, t // 2] = psum.tile([P, 2, QUARTER], F32, name="acc", bufs=8 - TBANKS)
                for s in range(4):
                    multiply(banks[g, q, t // 2][:, t % 2, :], ("sc", g, t), P * s, ("inc", q, s // 2), QUARTER * (s % 2), QUARTER, s == 0, s == 3)

        def scale_rows(g, q, u, slots):
            if (g, q) in NARROW:
                if len(slots) == 1 and u == 0:
                    return
                for e in range(2) if len(slots) == 1 else (u,):
                    if e == 0:
                        c_values[g, q] = flow.tile([P, QUARTER, 4], BF16, name="c_values", align_bytes=64)
                    nc.vector.tensor_tensor(out=c_values[g, q][:, P * e : P * (e + 1), :], in0=banks[g, q, e][:].rearrange("p t n -> p n t"),
                                            in1=row_gain[:, g, :].unsqueeze(1).to_broadcast([P, P, 4]), op=MULT)
                return
            gain = row_gain[:, g, 2 * u : 2 * u + 2].unsqueeze(1).to_broadcast([P, QUARTER, 2])
            src = banks[g, q, u][:].rearrange("p e n -> p n e")
            if DIRECT:
                if u == 0:
                    c_values[g, q] = flow.tile([P, QUARTER, 4], BF16, name="c_values", align_bytes=64)
                nc.vector.tensor_tensor(out=c_values[g, q][:, :, 2 * u : 2 * u + 2], in0=src, in1=gain, op=MULT)
            else:
                if u == 0:
                    c_pairs[g, q] = flow.tile([P, 2, QUARTER, 2], BF16, name="c_pairs", align_bytes=64)
                nc.vector.tensor_tensor(out=c_pairs[g, q][:, u], in0=src, in1=gain, op=MULT)

        def weave_c(g, q):
            if not DIRECT and (g, q) not in NARROW:
                c_values[g, q] = flow.tile([P, QUARTER, 4], BF16, name="c_values", align_bytes=64)
                dst = c_values[g, q][:].rearrange("p n t -> p (n t)").bitcast(F32).rearrange("p (n u) -> p n u", u=2)
                src = c_pairs[g, q][:].rearrange("p u n e -> p (u n e)").bitcast(F32).rearrange("p (u n) -> p n u", u=2)
                if WEAVE_SCALAR:
                    nc.scalar.copy(out=dst, in_=src)
                else:
                    nc.vector.tensor_copy(out=dst, in_=src)

        def quantize_c(g, q, half):
            key = ("c", g, q) if half is None else ("c", g, q, half)
            width = QUARTER if half is None else P
            codes[key] = keep.tile([P, width], U32, name="c_codes%d_%d_%s" % (g, q, half), align_bytes=64)
            scales[key] = keep.tile([P, width], U8, name="c_scales%d_%d_%s" % (g, q, half), align_bytes=64)
            cols = slice(0, QUARTER) if half is None else slice(P * half, P * (half + 1))
            nc.vector.quantize_mx(out=codes[key][:].bitcast(FP8X4), scales=scales[key][:],
                                  in_=c_values[g, q][:, cols, :].rearrange("p n t -> p (n t)"))

        products = {}

        def common(hs, q, half):
            width = QUARTER if half is None else P
            first = 0 if half is None else P * half
            bank = psum.tile([P, 2 * len(hs), width], F32, name="acc", bufs=8 - TBANKS)
            for n, h in enumerate(hs):
                for e in range(2):
                    for g in range(2):
                        if ("c", g, q) in codes:
                            multiply(bank[:, 2 * n + e, :], ("share", h), P * (2 * e + g), ("c", g, q), first, width, g == 0, g == 1)
                        else:
                            multiply(bank[:, 2 * n + e, :], ("share", h), P * (2 * e + g), ("c", g, q, half), 0, width, g == 0, g == 1)
            banks[hs, q, half] = bank

        def scale_columns(hs, q, half):
            width = QUARTER if half is None else P
            first = QUARTER * q + (0 if half is None else P * half)
            products[hs, q, half] = flow.tile([P, 2 * len(hs), width], F32, name="product", bufs=4)
            gain = col_gain[:, first : first + width].unsqueeze(1).to_broadcast([P, 2 * len(hs), width])
            nc.vector.tensor_tensor(out=products[hs, q, half][:], in0=banks[hs, q, half][:], in1=gain, op=MULT)

        def log_and_store(hs, q, half):
            width = QUARTER if half is None else P
            first = QUARTER * q + (0 if half is None else P * half)
            result = flow.tile([P, 2 * len(hs), width], F32, name="result", bufs=8)
            nc.scalar.activation(out=result[:], in_=products[hs, q, half][:], func=LN)
            for n, h in enumerate(hs):
                nc.sync.dma_start(out=out_rows[h, :, :, first : first + width], in_=result[:, 2 * n : 2 * n + 2, :])

        pending = []

        def defer(due, made, action, *args):
            pending.append((due, made, action, args))

        def release(now, needed):
            chain = [item[1][1:] for item in pending if item[1] in needed and item[1][0] == "c"]
            for item in list(pending):
                if item[0] <= now or item[1] in needed or (item[1][0] == "woven" and item[1][1:] in chain):
                    pending.remove(item)
                    item[2](*item[3])

        sorted_upto = max(UNSORTED, 1)
        if UNSORTED == 0:
            sort(0)
        for now, step in enumerate(steps):
            if step[0] == "overlap":
                g, q, slots = step[1:]
                both = (g, q) in NARROW and len(slots) > 1
                release(-1, [("sc", g, t) for t in (range(4) if both else slots)] + [("inc", q, 0), ("inc", q, 1)])
                overlap(g, q, slots)
            if step[0] == "common":
                release(-1, [("share", h) for h in step[1]] + [("c", 0, step[2]), ("c", 1, step[2]), ("c", 1, step[2], step[3])])
                common(step[1], step[2], step[3])
            if step[0] == "turn":
                turn(step[1])
            release(now, [])
            if step[0] == "turn":
                defer(now + LAG_Q, step[1], quantize_input, step[1])
                turned = turns.index(step[1]) + 1
                if WARM and turns.index(step[1]) in WARM_FILL:
                    warm_up(FILL)
            sorted_upto = max(sorted_upto, turned)
            while sorted_upto in SKIP:
                sorted_upto = sorted_upto + 1
            if sorted_upto < min(turned + (1 if turned < HEAD else SORT_AHEAD), len(turns)) and (step[0] != "turn" or ((turned > UNSORTED or WARM) and sorted_upto not in SCALAR_SORTS)):
                if sorted_upto not in SKIP:
                    sort(sorted_upto)
                sorted_upto = sorted_upto + 1
            if step[0] == "overlap" and slots[-1] % 2 == 1:
                scale_rows(g, q, slots[-1] // 2, slots)
            if step[0] == "overlap" and SPLIT_LAST and (g, q) == (1, 3):
                defer(now + LAG_C, ("c", g, q, slots[-1] // 2), quantize_c, g, q, slots[-1] // 2)
            elif step[0] == "overlap" and slots[-1] == 3:
                if (g, q) in NARROW:
                    defer(now + LAG_C, ("c", g, q), quantize_c, g, q, None)
                else:
                    defer(now + LAG_C, ("woven", g, q), weave_c, g, q)
                    defer(now + LAG_C + 1, ("c", g, q), quantize_c, g, q, None)
            if step[0] == "common":
                scale_columns(step[1], step[2], step[3])
                defer(now + LAG_LOG, ("out",) + step[1:], log_and_store, step[1], step[2], step[3])
        release(len(steps) + 9, [])
